import numpy as np
import ml_dtypes


def mxq(x, axis, fmt="e4m3"):
    dtype, down = {"e4m3": (ml_dtypes.float8_e4m3fn, 7), "e5m2": (ml_dtypes.float8_e5m2, 14)}[fmt]
    v = np.moveaxis(np.asarray(x, np.float32).astype(ml_dtypes.bfloat16).astype(np.float64), axis, -1)
    blocks = v.reshape(v.shape[:-1] + (-1, 32))
    amax = np.abs(blocks).max(-1, keepdims=True)
    byte = np.maximum(np.where(amax > 0, np.frexp(amax)[1] - 1 + 127, 0) - down, 1)
    scale = np.exp2(byte - 127.0)
    codes = (blocks / scale).astype(np.float32).astype(dtype).astype(np.float64)
    return np.moveaxis((codes * scale).reshape(v.shape), -1, axis)


WIDE = False


def mx_kscale(k):
    if not WIDE:
        return np.ones(k)
    levels = np.array([10, -10, 5, -5, 0])
    if k % 512:
        return np.exp2(np.random.permutation(np.resize(levels, k // 32))).repeat(32)
    a = np.empty((k // 512, 16))
    for p in range(k // 512):
        a[p, :8] = np.random.permutation(np.resize(levels, 8))
        for g in range(8):
            far = levels[np.abs(levels - a[p, g]) >= 10]
            a[p, g + 8] = far[np.random.randint(len(far))]
    return np.exp2(a.ravel()).repeat(32)


def f64(x):
    return np.asarray(x).astype(np.float64)


def striped(idx):
    return np.tile(idx.reshape(-1, 16).T, (8, 1)).astype(np.uint16)


def unstriped(offs):
    return offs[:16].T.reshape(-1).astype(np.int64)


def pack_weight(w):
    k, n = w.shape
    w = f64(np.asarray(w, np.float32).astype(ml_dtypes.bfloat16)).reshape(k // 32, 32, n)
    amax = np.abs(w).max(1)
    byte = np.clip(np.where(amax > 0, np.frexp(amax)[1] - 1 + 127 - 7, 1), 1, 254)
    scaled = (w * np.exp2(127.0 - byte)[:, None, :]).reshape(k, n).astype(np.float32)
    words = np.ascontiguousarray(scaled.reshape(k // 512, 128, 4, n).transpose(0, 1, 3, 2)).astype(ml_dtypes.float8_e4m3fn).view(np.uint8)
    return words, np.ascontiguousarray(byte.astype(np.uint8).reshape(k // 512, 16, n))


def unpack_weight(words, scales):
    g, p, n, _ = words.shape
    vals = np.ascontiguousarray(words).view(ml_dtypes.float8_e4m3fn).astype(np.float64) * np.repeat(np.exp2(scales.astype(np.float64) - 127.0), 8, axis=1)[..., None]
    return vals.transpose(0, 1, 3, 2).reshape(g * 512, n)


K, T, S, N, H, U = 512, 2048, 512, 128, 512, 1024


def setup_inputs():
    n = np.random.standard_normal
    s = mx_kscale(K)[:, None]
    u = mx_kscale(H)
    packed_xT = pack_weight(n((K, T)) * s)
    return {
        "x_words": packed_xT[0],
        "x_scales": packed_xT[1],
        "w1": (n((K, H)) / np.sqrt(K) / s).astype(np.float32),
        "w2": (n((K, H)) / np.sqrt(K) / s).astype(np.float32),
        "sca": (np.random.uniform(0.6, 1.4, (H, U))).astype(np.float32),
        "unit": (np.random.uniform(0.6, 1.4, (H, 1)) * u[:, None]).astype(np.float32),
        "w3": (n((H, N)) / np.sqrt(H) / u[:, None]).astype(np.float32),
        "offs": striped(np.random.permutation(T)[:S]),
        "va": striped(np.random.permutation(np.concatenate([np.arange(S), np.random.randint(0, S, U - S)]))),
        "vb": striped(np.random.permutation(np.concatenate([np.arange(S), np.random.randint(0, S, U - S)]))),
    }


def reference(x_words, x_scales, w1, w2, sca, unit, w3, offs, va, vb):
    xq = unpack_weight(x_words, x_scales)[:, unstriped(offs)]
    cf = mxq(f64(w2), 0, "e4m3").T @ xq
    conf = np.exp(1.2 * np.tanh(cf)) + 0.5
    ca = conf[:, unstriped(va)]
    cb = conf[:, unstriped(vb)]
    wp = ca * cb
    px = mxq(f64(w1), 0, "e4m3").T @ xq
    xa = px[:, unstriped(va)]
    xb = px[:, unstriped(vb)]
    res = f64(sca) * xa - xb
    hub = res / (np.sqrt((res) ** 2 + 0.3))
    gr = wp * hub
    hid = f64(unit) * gr
    return mxq(f64(w3), 0, "e4m3").T @ mxq(hid, 0, "e4m3")

@@ -1,0 +1,291 @@
+from contextlib import ExitStack
+
+import concourse.mybir as mybir
+from concourse.masks import make_identity
+
+K, T, S, N, H, U = 512, 2048, 512, 128, 512, 1024
+FLOPS = 2 * K * H * S * 2 + 2 * H * N * U
+
+F32 = mybir.dt.float32
+BF16 = mybir.dt.bfloat16
+I32 = mybir.dt.int32
+U32 = mybir.dt.uint32
+U16 = mybir.dt.uint16
+U8 = mybir.dt.uint8
+FP8X4 = mybir.dt.float8_e4m3fn_x4
+ACT = mybir.ActivationFunctionType
+ALU = mybir.AluOpType
+
+P = 128
+PACK = 4
+TILES = H // P
+WINDOW = S + 16
+CHUNKS = (512, 512)
+PIECES2 = (256, 256)
+PIECES1 = (256, 256)
+LAG_SQ = 1
+LAG_HUB = 2
+LAG_WP = 1
+RING = 3
+RES_BANKS = 3
+WP_BANKS = 2
+TURN_BANKS = 2
+GROUP = 256
+E_MEMSET = "gpsimd"
+E_PX = "vvvv"
+E_W = {"w2_0": "s", "w2_1": "v", "w1_0": "v", "w1_1": "v", "w3_0": "v", "w2_2": "v", "w1_2": "v", "w2_3": "v", "w1_3": "v"}
+E_CONF = "vector"
+E_TURN = "vvvvvvss"
+E_OUT = "ssssssss"
+LOADS = ("offs", "bytes", "words", "w2_0", "w1_0", "va", "vb", "unit", "w2_1", "sca_0_0", "w1_1", "sca_0_1", "sca_0_2", "sca_0_3", "w3_0")
+
+
+def tile_picked_ydustr_grad_p_kernel(
+    tc, x_words, x_scales, w1, w2, sca, unit, w3, offs, va, vb, out
+):
+    nc = tc.nc
+    engines = {"gpsimd": nc.gpsimd, "vector": nc.vector}
+
+    def copy_on(letter, dst, src):
+        if letter == "v":
+            nc.vector.tensor_copy(dst, src)
+        else:
+            nc.scalar.copy(dst, src)
+
+    with ExitStack() as ctx:
+        keep = ctx.enter_context(tc.tile_pool(name="keep", bufs=1))
+        ring = ctx.enter_context(tc.tile_pool(name="ring", bufs=RING))
+        psum = ctx.enter_context(tc.psum_pool(name="psum", bufs=1))
+
+        offs_sb = keep.tile([P, S // 16], U16, name="offs_sb")
+        va_sb = keep.tile([P, U // 16], U16, name="va_sb")
+        vb_sb = keep.tile([P, U // 16], U16, name="vb_sb")
+        words_all = keep.tile([P, T], I32, name="words_all", align_bytes=64)
+        bytes_all = keep.tile([P, T], U8, name="bytes_all", align_bytes=64)
+        unit_sb = keep.tile([P, TILES], F32, name="unit_sb")
+        engines[E_MEMSET].memset(bytes_all[:].bitcast(I32), 0)
+
+        starts = [sum(CHUNKS[:c]) for c in range(len(CHUNKS))]
+        pieces = {"w3_0": (w3, 0, N)}
+        for name, w, widths in (("w2", w2, PIECES2), ("w1", w1, PIECES1)):
+            for n, width in enumerate(widths):
+                pieces["%s_%d" % (name, n)] = (w, sum(widths[:n]), width)
+        raw = {}
+        sca_sb = {}
+
+        def load(name):
+            if name == "offs":
+                nc.sync.dma_start(offs_sb[:], offs)
+            elif name == "va":
+                nc.sync.dma_start(va_sb[:], va)
+            elif name == "vb":
+                nc.sync.dma_start(vb_sb[:], vb)
+            elif name == "words":
+                nc.sync.dma_start(words_all[:], x_words[0].rearrange("p n t -> p (n t)").bitcast(I32))
+            elif name == "bytes":
+                for q in range(4):
+                    nc.sync.dma_start(
+                        bytes_all[32 * q : 32 * q + 4, :].bitcast(I32), x_scales[0, 4 * q : 4 * q + 4, :].bitcast(I32)
+                    )
+            elif name == "unit":
+                with nc.allow_non_contiguous_dma(reason="one value a partition and tile"):
+                    nc.sync.dma_start(unit_sb[:], unit.rearrange("(t p) o -> p (t o)", p=P))
+            elif name in pieces:
+                w, col0, width = pieces[name]
+                raw[name] = keep.tile([P, PACK, width], F32, name="raw_" + name)
+                nc.sync.dma_start(raw[name][:], w[:, col0 : col0 + width].rearrange("(p j) c -> p j c", j=PACK))
+            else:
+                c, t = int(name.split("_")[1]), int(name.split("_")[2])
+                sca_sb[c, t] = keep.tile([P, CHUNKS[c]], F32, name=name)
+                nc.sync.dma_start(sca_sb[c, t][:], sca[t * P : (t + 1) * P, starts[c] : starts[c] + CHUNKS[c]])
+
+        for name in LOADS:
+            load(name)
+        for c in range(1, len(CHUNKS)):
+            for t in range(TILES):
+                load("sca_%d_%d" % (c, t))
+
+        ident = keep.tile([P, P], F32, name="ident")
+        make_identity(nc, ident[:])
+
+        def window(name):
+            tile = keep.tile([P, WINDOW], F32, name=name)
+            nc.gpsimd.memset(tile[:, S:], 0.0)
+            return tile
+
+        e_tab = [window("e_tab%d" % t) for t in range(TILES)]
+        conf_tab = [window("conf_tab%d" % t) for t in range(TILES)]
+        px_tab = [window("px_tab%d" % t) for t in range(TILES)]
+
+        x_codes = keep.tile([P, S], U32, name="x_codes", align_bytes=64)
+        x_bytes = keep.tile([P, S], U8, name="x_bytes", align_bytes=64)
+        nc.vector.tensor_copy(x_bytes[:], bytes_all[:].indirect(offs_sb[:]))
+        nc.vector.tensor_copy(x_codes[:], words_all[:].bitcast(U32).indirect(offs_sb[:]))
+
+        quantised = {}
+
+        def quantise_weight(name):
+            width = pieces[name][2]
+            grouped = keep.tile([P, width, PACK], BF16, name="grouped_" + name, align_bytes=64)
+            copy_on(
+                E_W[name],
+                grouped[:].rearrange("p (c i) j -> p c j i", i=4),
+                raw[name][:].rearrange("p j (c i) -> p c j i", i=4),
+            )
+            codes = keep.tile([P, width], U32, name="codes_" + name, align_bytes=64)
+            scales = keep.tile([P, width], U8, name="scales_" + name, align_bytes=64)
+            nc.vector.quantize_mx(
+                out=codes[:].bitcast(FP8X4), scales=scales[:], in_=grouped[:].rearrange("p c j -> p (c j)")
+            )
+            quantised[name] = (codes, scales)
+
+        def first_product(matrix, t, tag, bufs):
+            name = [n for n in pieces if n.startswith(matrix) and pieces[n][1] <= t * P < pieces[n][1] + pieces[n][2]][0]
+            if name not in quantised:
+                quantise_weight(name)
+            codes, scales = quantised[name]
+            cols = slice(t * P - pieces[name][1], (t + 1) * P - pieces[name][1])
+            acc = psum.tile([P, S], F32, name="acc", tag=tag, bufs=bufs)
+            nc.tensor.matmul_mx(
+                out=acc[:],
+                lhsT=codes[:, cols].bitcast(FP8X4),
+                lhsT_scale=scales[:, cols],
+                rhs=x_codes[:].bitcast(FP8X4),
+                rhs_scale=x_bytes[:],
+                start=True,
+                stop=True,
+            )
+            return acc
+
+        for t in range(TILES):
+            cf = first_product("w2", t, "res", RES_BANKS)
+            th = ring.tile([P, S], F32, name="th")
+            nc.scalar.activation(th[:], cf[:], ACT.Tanh)
+            nc.scalar.activation(e_tab[t][:, :S], th[:], ACT.Exp, scale=1.2)
+            px = first_product("w1", t, "wp", WP_BANKS)
+            copy_on(E_PX[t], px_tab[t][:, :S], px[:])
+            engines[E_CONF].tensor_scalar(
+                conf_tab[t][:, :S], e_tab[t][:, :S], 0.5, unit_sb[:, t : t + 1], ALU.add, ALU.mult
+            )
+        quantise_weight("w3_0")
+        w3_codes, w3_scales = quantised["w3_0"]
+
+        units = [(c, t) for c in range(len(CHUNKS)) for t in range(TILES)]
+        hid_t = [keep.tile([P, CHUNKS[c] // P, H], BF16, name="hid_t%d" % c) for c in range(len(CHUNKS))]
+        state = {}
+
+        def entries(lst, c):
+            return lst[:, starts[c] // 16 : (starts[c] + CHUNKS[c]) // 16]
+
+        def fetch_a(k):
+            c, t = units[k]
+            ca = ring.tile([P, CHUNKS[c]], F32, name="ca")
+            nc.scalar.activation(ca[:], e_tab[t][:].indirect(entries(va_sb, c)), ACT.Copy, bias=0.5)
+            sxa = ring.tile([P, CHUNKS[c]], F32, name="sxa")
+            nc.vector.tensor_tensor(sxa[:], px_tab[t][:].indirect(entries(va_sb, c)), sca_sb[c, t][:], ALU.mult)
+            state["ca", k], state["sxa", k] = ca, sxa
+
+        def fetch_b(k):
+            c, t = units[k]
+            nxb = ring.tile([P, CHUNKS[c]], F32, name="nxb")
+            nc.scalar.activation(nxb[:], px_tab[t][:].indirect(entries(vb_sb, c)), ACT.Copy, scale=-1.0)
+            wp = ring.tile([P, CHUNKS[c]], F32, name="wp")
+            nc.vector.tensor_tensor(wp[:], conf_tab[t][:].indirect(entries(vb_sb, c)), state["ca", k][:], ALU.mult)
+            state["wp", k], state["nxb", k] = wp, nxb
+
+        def turn_res(k):
+            width = CHUNKS[units[k][0]]
+            res = psum.tile([P, width], F32, name="res", tag="res", bufs=RES_BANKS)
+            for b in range(width // P):
+                cols = slice(b * P, (b + 1) * P)
+                nc.tensor.matmul(res[:, cols], state["sxa", k][:, cols], ident[:], start=True, stop=False, is_transpose=True)
+                nc.tensor.matmul(res[:, cols], state["nxb", k][:, cols], ident[:], start=False, stop=True, is_transpose=True)
+            state["res", k] = res
+
+        def turn_wp(k):
+            width = CHUNKS[units[k][0]]
+            wp_t = psum.tile([P, width], F32, name="wp_t", tag="wp", bufs=WP_BANKS)
+            for b in range(width // P):
+                cols = slice(b * P, (b + 1) * P)
+                nc.tensor.transpose(wp_t[:, cols], state["wp", k][:, cols], ident[:])
+            state["wp_t", k] = wp_t
+
+        def square(k):
+            sq = ring.tile([P, CHUNKS[units[k][0]]], F32, name="sq")
+            nc.scalar.activation(sq[:], state["res", k][:], ACT.Square)
+            state["sq", k] = sq
+
+        def inverse_root(k):
+            rs = ring.tile([P, CHUNKS[units[k][0]]], F32, name="rs")
+            nc.scalar.activation(rs[:], state["sq", k][:], ACT.Abs_reciprocal_sqrt, bias=0.3)
+            state["rs", k] = rs
+
+        def huber(k):
+            hub = ring.tile([P, CHUNKS[units[k][0]]], F32, name="hub")
+            nc.vector.tensor_tensor(hub[:], state["res", k][:], state["rs", k][:], ALU.mult)
+            state["hub", k] = hub
+
+        def hidden(k):
+            c, t = units[k]
+            nc.vector.tensor_tensor(
+                hid_t[c][:, :, t * P : (t + 1) * P],
+                state["wp_t", k][:].rearrange("p (b i) -> p b i", i=P),
+                state["hub", k][:].rearrange("p (b i) -> p b i", i=P),
+                ALU.mult,
+            )
+
+        def last_product(c, col0, width):
+            group = (starts[c] + col0) // P
+            blocks = width // P
+            grouped = ring.tile([P, width, PACK], BF16, name="hid_grouped", align_bytes=64)
+            grouped_words = grouped[:].rearrange("p r j -> p (r j)").bitcast(F32)
+            turned = psum.tile([P, blocks, 2, P], F32, name="turned", tag="turned", bufs=TURN_BANKS)
+            for b in range(blocks):
+                words = hid_t[c][:, col0 // P + b, :].bitcast(F32)
+                for u in range(2):
+                    nc.tensor.transpose(turned[:, b, u, :], words[:, u::2], ident[:])
+            copy_on(
+                E_TURN[group],
+                grouped_words.rearrange("p (b r u) -> p b r u", b=blocks, u=2),
+                turned[:].rearrange("p b u r -> p b r u"),
+            )
+            codes = ring.tile([P, width], U32, name="hid_codes", align_bytes=64)
+            scales = ring.tile([P, width], U8, name="hid_scales", align_bytes=64)
+            nc.vector.quantize_mx(
+                out=codes[:].bitcast(FP8X4), scales=scales[:], in_=grouped[:].rearrange("p r j -> p (r j)")
+            )
+            acc = psum.tile([P, width], F32, name="out_acc", tag="out", bufs=8 - RES_BANKS - WP_BANKS - TURN_BANKS)
+            nc.tensor.matmul_mx(
+                out=acc[:],
+                lhsT=w3_codes[:].bitcast(FP8X4),
+                lhsT_scale=w3_scales[:],
+                rhs=codes[:].bitcast(FP8X4),
+                rhs_scale=scales[:],
+                start=True,
+                stop=True,
+            )
+            result = ring.tile([P, width], F32, name="result")
+            copy_on(E_OUT[group], result[:], acc[:])
+            nc.sync.dma_start(out[:, starts[c] + col0 : starts[c] + col0 + width], result[:])
+
+        count = len(units)
+        for step in range(count + LAG_HUB):
+            if step < count:
+                fetch_a(step)
+            if 0 <= step - LAG_SQ < count:
+                turn_res(step - LAG_SQ)
+                square(step - LAG_SQ)
+            if step >= LAG_HUB:
+                huber(step - LAG_HUB)
+            if step < count:
+                fetch_b(step)
+            if 0 <= step - LAG_WP < count:
+                turn_wp(step - LAG_WP)
+            if 0 <= step - LAG_SQ < count:
+                inverse_root(step - LAG_SQ)
+            if step >= LAG_HUB:
+                hidden(step - LAG_HUB)
+                c, t = units[step - LAG_HUB]
+                if t == TILES - 1:
+                    for col0 in range(0, CHUNKS[c], GROUP):
+                        last_product(c, col0, min(GROUP, CHUNKS[c] - col0))

@@ -25,17 +25,34 @@ PIECES2 = (256, 256)
 PIECES1 = (256, 256)
 LAG_SQ = 1
 LAG_HUB = 2
-LAG_WP = 1
-RING = 3
+LAG_WP = 2
+RING = 4
 RES_BANKS = 3
 WP_BANKS = 2
 TURN_BANKS = 2
 GROUP = 256
+LAST_GROUP = 128
+SPLIT = 1
+LAST_PIECE = 256
+LAG_RES = 1
+LAG_HID = 3
+POST = 3
+TOGETHER = 0
+HID_SPAN = 256
+OUT_BANKS = 1
+TAGS_LAST = ("res", "turned")
+TAGS_FIRST = ("turned", "out")
+TAG2 = "res"
+TAG1 = "wp"
+UNITS = ((0, 0), (0, 1), (0, 2), (0, 3), (1, 0), (1, 1), (1, 2), (1, 3))
+Q_BYTES = ("sync", "sync", "sync", "sync")
+DEFER = 1
+EARLY = 0
 E_MEMSET = "gpsimd"
 E_PX = "vvvv"
 E_W = {"w2_0": "s", "w2_1": "v", "w1_0": "v", "w1_1": "v", "w3_0": "v", "w2_2": "v", "w1_2": "v", "w2_3": "v", "w1_3": "v"}
 E_CONF = "vector"
-E_TURN = "vvvvvvss"
+E_TURN = "ssvvvsvs"
 E_OUT = "ssssssss"
 LOADS = ("offs", "bytes", "words", "w2_0", "w1_0", "va", "vb", "unit", "w2_1", "sca_0_0", "w1_1", "sca_0_1", "sca_0_2", "sca_0_3", "w3_0")
 
@@ -44,7 +61,7 @@ def tile_picked_ydustr_grad_p_kernel(
     tc, x_words, x_scales, w1, w2, sca, unit, w3, offs, va, vb, out
 ):
     nc = tc.nc
-    engines = {"gpsimd": nc.gpsimd, "vector": nc.vector}
+    engines = {"gpsimd": nc.gpsimd, "vector": nc.vector, "scalar": nc.scalar, "sync": nc.sync}
 
     def copy_on(letter, dst, src):
         if letter == "v":
@@ -55,6 +72,7 @@ def tile_picked_ydustr_grad_p_kernel(
     with ExitStack() as ctx:
         keep = ctx.enter_context(tc.tile_pool(name="keep", bufs=1))
         ring = ctx.enter_context(tc.tile_pool(name="ring", bufs=RING))
+        post = ctx.enter_context(tc.tile_pool(name="post", bufs=POST))
         psum = ctx.enter_context(tc.psum_pool(name="psum", bufs=1))
 
         offs_sb = keep.tile([P, S // 16], U16, name="offs_sb")
@@ -84,7 +102,7 @@ def tile_picked_ydustr_grad_p_kernel(
                 nc.sync.dma_start(words_all[:], x_words[0].rearrange("p n t -> p (n t)").bitcast(I32))
             elif name == "bytes":
                 for q in range(4):
-                    nc.sync.dma_start(
+                    engines[Q_BYTES[q]].dma_start(
                         bytes_all[32 * q : 32 * q + 4, :].bitcast(I32), x_scales[0, 4 * q : 4 * q + 4, :].bitcast(I32)
                     )
             elif name == "unit":
@@ -101,8 +119,8 @@ def tile_picked_ydustr_grad_p_kernel(
 
         for name in LOADS:
             load(name)
-        for c in range(1, len(CHUNKS)):
-            for t in range(TILES):
+        for c, t in UNITS:
+            if (c, t) not in sca_sb:
                 load("sca_%d_%d" % (c, t))
 
         ident = keep.tile([P, P], F32, name="ident")
@@ -123,6 +141,7 @@ def tile_picked_ydustr_grad_p_kernel(
         nc.vector.tensor_copy(x_codes[:], words_all[:].bitcast(U32).indirect(offs_sb[:]))
 
         quantised = {}
+        banks = {"res": RES_BANKS, "wp": WP_BANKS, "turned": TURN_BANKS, "out": OUT_BANKS}
 
         def quantise_weight(name):
             width = pieces[name][2]
@@ -158,11 +177,11 @@ def tile_picked_ydustr_grad_p_kernel(
             return acc
 
         for t in range(TILES):
-            cf = first_product("w2", t, "res", RES_BANKS)
+            cf = first_product("w2", t, TAG2, banks[TAG2])
             th = ring.tile([P, S], F32, name="th")
             nc.scalar.activation(th[:], cf[:], ACT.Tanh)
             nc.scalar.activation(e_tab[t][:, :S], th[:], ACT.Exp, scale=1.2)
-            px = first_product("w1", t, "wp", WP_BANKS)
+            px = first_product("w1", t, TAG1, banks[TAG1])
             copy_on(E_PX[t], px_tab[t][:, :S], px[:])
             engines[E_CONF].tensor_scalar(
                 conf_tab[t][:, :S], e_tab[t][:, :S], 0.5, unit_sb[:, t : t + 1], ALU.add, ALU.mult
@@ -170,9 +189,14 @@ def tile_picked_ydustr_grad_p_kernel(
         quantise_weight("w3_0")
         w3_codes, w3_scales = quantised["w3_0"]
 
-        units = [(c, t) for c in range(len(CHUNKS)) for t in range(TILES)]
-        hid_t = [keep.tile([P, CHUNKS[c] // P, H], BF16, name="hid_t%d" % c) for c in range(len(CHUNKS))]
+        units = list(UNITS)
+        spans = [CHUNKS[c] if c < len(CHUNKS) - 1 else HID_SPAN for c in range(len(CHUNKS))]
+        hid_t = {}
+        for c in range(len(CHUNKS)):
+            for col0 in range(0, CHUNKS[c], spans[c]):
+                hid_t[c, col0] = keep.tile([P, spans[c] // P, H], BF16, name="hid_t%d_%d" % (c, col0))
         state = {}
+        waiting = []
 
         def entries(lst, c):
             return lst[:, starts[c] // 16 : (starts[c] + CHUNKS[c]) // 16]
@@ -193,55 +217,78 @@ def tile_picked_ydustr_grad_p_kernel(
             nc.vector.tensor_tensor(wp[:], conf_tab[t][:].indirect(entries(vb_sb, c)), state["ca", k][:], ALU.mult)
             state["wp", k], state["nxb", k] = wp, nxb
 
-        def turn_res(k):
+        def parts(k):
             width = CHUNKS[units[k][0]]
+            piece = LAST_PIECE if k >= len(units) - SPLIT else width
+            return [(k, col0, min(piece, width - col0)) for col0 in range(0, width, piece)]
+
+        def turn_res(part):
+            k, col0, width = part
             res = psum.tile([P, width], F32, name="res", tag="res", bufs=RES_BANKS)
             for b in range(width // P):
                 cols = slice(b * P, (b + 1) * P)
-                nc.tensor.matmul(res[:, cols], state["sxa", k][:, cols], ident[:], start=True, stop=False, is_transpose=True)
-                nc.tensor.matmul(res[:, cols], state["nxb", k][:, cols], ident[:], start=False, stop=True, is_transpose=True)
-            state["res", k] = res
+                src = slice(col0 + b * P, col0 + (b + 1) * P)
+                nc.tensor.matmul(res[:, cols], state["sxa", k][:, src], ident[:], start=True, stop=False, is_transpose=True)
+                nc.tensor.matmul(res[:, cols], state["nxb", k][:, src], ident[:], start=False, stop=True, is_transpose=True)
+            state["res", part] = res
 
-        def turn_wp(k):
-            width = CHUNKS[units[k][0]]
+        def turn_wp(part):
+            k, col0, width = part
             wp_t = psum.tile([P, width], F32, name="wp_t", tag="wp", bufs=WP_BANKS)
             for b in range(width // P):
-                cols = slice(b * P, (b + 1) * P)
-                nc.tensor.transpose(wp_t[:, cols], state["wp", k][:, cols], ident[:])
-            state["wp_t", k] = wp_t
+                nc.tensor.transpose(wp_t[:, b * P : (b + 1) * P], state["wp", k][:, col0 + b * P : col0 + (b + 1) * P], ident[:])
+            state["wp_t", part] = wp_t
 
-        def square(k):
-            sq = ring.tile([P, CHUNKS[units[k][0]]], F32, name="sq")
-            nc.scalar.activation(sq[:], state["res", k][:], ACT.Square)
-            state["sq", k] = sq
+        def square(part):
+            sq = post.tile([P, part[2]], F32, name="sq")
+            nc.scalar.activation(sq[:], state["res", part][:], ACT.Square)
+            state["sq", part] = sq
 
-        def inverse_root(k):
-            rs = ring.tile([P, CHUNKS[units[k][0]]], F32, name="rs")
-            nc.scalar.activation(rs[:], state["sq", k][:], ACT.Abs_reciprocal_sqrt, bias=0.3)
-            state["rs", k] = rs
+        def inverse_root(part):
+            rs = post.tile([P, part[2]], F32, name="rs")
+            nc.scalar.activation(rs[:], state["sq", part][:], ACT.Abs_reciprocal_sqrt, bias=0.3)
+            state["rs", part] = rs
 
-        def huber(k):
-            hub = ring.tile([P, CHUNKS[units[k][0]]], F32, name="hub")
-            nc.vector.tensor_tensor(hub[:], state["res", k][:], state["rs", k][:], ALU.mult)
-            state["hub", k] = hub
+        def huber(part):
+            hub = post.tile([P, part[2]], F32, name="hub")
+            nc.vector.tensor_tensor(hub[:], state["res", part][:], state["rs", part][:], ALU.mult)
+            state["hub", part] = hub
 
-        def hidden(k):
+        def hidden(part):
+            k, col0, width = part
             c, t = units[k]
-            nc.vector.tensor_tensor(
-                hid_t[c][:, :, t * P : (t + 1) * P],
-                state["wp_t", k][:].rearrange("p (b i) -> p b i", i=P),
-                state["hub", k][:].rearrange("p (b i) -> p b i", i=P),
-                ALU.mult,
-            )
+            step = min(width, spans[c])
+            for at in range(0, width, step):
+                base = (col0 + at) // spans[c] * spans[c]
+                first = (col0 + at - base) // P
+                nc.vector.tensor_tensor(
+                    hid_t[c, base][:, first : first + step // P, t * P : (t + 1) * P],
+                    state["wp_t", part][:, at : at + step].rearrange("p (b i) -> p b i", i=P),
+                    state["hub", part][:, at : at + step].rearrange("p (b i) -> p b i", i=P),
+                    ALU.mult,
+                )
+
+        def finish(part):
+            k, col0, width = part
+            c, t = units[k]
+            if t == TILES - 1:
+                group = GROUP if c < len(CHUNKS) - 1 else LAST_GROUP
+                for g0 in range(col0, col0 + width, group):
+                    if c < len(CHUNKS) - 1:
+                        waiting.append((k + DEFER, c, g0, min(group, col0 + width - g0)))
+                    else:
+                        last_product(c, g0, min(group, col0 + width - g0))
 
         def last_product(c, col0, width):
             group = (starts[c] + col0) // P
             blocks = width // P
+            tag_turn, tag_out = TAGS_LAST if c == len(CHUNKS) - 1 else TAGS_FIRST
             grouped = ring.tile([P, width, PACK], BF16, name="hid_grouped", align_bytes=64)
             grouped_words = grouped[:].rearrange("p r j -> p (r j)").bitcast(F32)
-            turned = psum.tile([P, blocks, 2, P], F32, name="turned", tag="turned", bufs=TURN_BANKS)
+            turned = psum.tile([P, blocks, 2, P], F32, name="turned", tag=tag_turn, bufs=banks[tag_turn])
             for b in range(blocks):
-                words = hid_t[c][:, col0 // P + b, :].bitcast(F32)
+                base = col0 // spans[c] * spans[c]
+                words = hid_t[c, base][:, (col0 - base) // P + b, :].bitcast(F32)
                 for u in range(2):
                     nc.tensor.transpose(turned[:, b, u, :], words[:, u::2], ident[:])
             copy_on(
@@ -254,7 +301,7 @@ def tile_picked_ydustr_grad_p_kernel(
             nc.vector.quantize_mx(
                 out=codes[:].bitcast(FP8X4), scales=scales[:], in_=grouped[:].rearrange("p r j -> p (r j)")
             )
-            acc = psum.tile([P, width], F32, name="out_acc", tag="out", bufs=8 - RES_BANKS - WP_BANKS - TURN_BANKS)
+            acc = psum.tile([P, width], F32, name="out_acc", tag=tag_out, bufs=banks[tag_out])
             nc.tensor.matmul_mx(
                 out=acc[:],
                 lhsT=w3_codes[:].bitcast(FP8X4),
@@ -269,23 +316,30 @@ def tile_picked_ydustr_grad_p_kernel(
             nc.sync.dma_start(out[:, starts[c] + col0 : starts[c] + col0 + width], result[:])
 
         count = len(units)
-        for step in range(count + LAG_HUB):
+
+        def each(stage, k):
+            if 0 <= k < count:
+                for part in parts(k):
+                    stage(part)
+
+        for step in range(count + LAG_HID):
             if step < count:
                 fetch_a(step)
-            if 0 <= step - LAG_SQ < count:
-                turn_res(step - LAG_SQ)
-                square(step - LAG_SQ)
-            if step >= LAG_HUB:
-                huber(step - LAG_HUB)
+            each(turn_res, step - LAG_RES)
+            each(square, step - LAG_SQ)
+            each(huber, step - LAG_HUB)
             if step < count:
                 fetch_b(step)
-            if 0 <= step - LAG_WP < count:
-                turn_wp(step - LAG_WP)
-            if 0 <= step - LAG_SQ < count:
-                inverse_root(step - LAG_SQ)
-            if step >= LAG_HUB:
-                hidden(step - LAG_HUB)
-                c, t = units[step - LAG_HUB]
-                if t == TILES - 1:
-                    for col0 in range(0, CHUNKS[c], GROUP):
-                        last_product(c, col0, min(GROUP, CHUNKS[c] - col0))
+            each(turn_wp, step - LAG_WP)
+            each(inverse_root, step - LAG_SQ)
+            for item in list(waiting):
+                if item[0] <= step - LAG_HID + EARLY:
+                    waiting.remove(item)
+                    last_product(*item[1:])
+            if TOGETHER:
+                each(hidden, step - LAG_HID)
+                each(finish, step - LAG_HID)
+            elif 0 <= step - LAG_HID < count:
+                for part in parts(step - LAG_HID):
+                    hidden(part)
+                    finish(part)

@@ -49,12 +49,12 @@ Q_BYTES = ("sync", "sync", "sync", "sync")
 DEFER = 1
 EARLY = 0
 E_MEMSET = "gpsimd"
-E_PX = "vvvv"
+E_PX = "svvv"
 E_W = {"w2_0": "s", "w2_1": "v", "w1_0": "v", "w1_1": "v", "w3_0": "v", "w2_2": "v", "w1_2": "v", "w2_3": "v", "w1_3": "v"}
 E_CONF = "vector"
 E_TURN = "ssvvvsvs"
 E_OUT = "ssssssss"
-LOADS = ("offs", "bytes", "words", "w2_0", "w1_0", "va", "vb", "unit", "w2_1", "sca_0_0", "w1_1", "sca_0_1", "sca_0_2", "sca_0_3", "w3_0")
+LOADS = ("offs", "w2_0", "bytes", "words", "w2_1", "va", "w1_0", "vb", "unit", "sca_0_0", "w1_1", "sca_0_1", "sca_0_2", "sca_0_3", "w3_0")
 
 
 def tile_picked_ydustr_grad_p_kernel(

@@ -18,281 +18,239 @@ ALU = mybir.AluOpType
 
 P = 128
 PACK = 4
+LIST_ROWS = 16
 TILES = H // P
+CHUNK = 512
+CHUNKS = U // CHUNK
+HALF = CHUNK // 2
+WEIGHT_HALF = H // 2
 WINDOW = S + 16
-CHUNKS = (512, 512)
-PIECES2 = (256, 256)
-PIECES1 = (256, 256)
-LAG_SQ = 1
-LAG_HUB = 2
-LAG_WP = 2
-RING = 4
-RES_BANKS = 3
-WP_BANKS = 2
-TURN_BANKS = 2
-GROUP = 256
-LAST_GROUP = 128
-SPLIT = 1
-LAST_PIECE = 256
-LAG_RES = 1
+
+LAG_ROOT = 1
+LAG_CLIP = 2
 LAG_HID = 3
-POST = 3
-TOGETHER = 0
-HID_SPAN = 256
-OUT_BANKS = 1
-TAGS_LAST = ("res", "turned")
-TAGS_FIRST = ("turned", "out")
-TAG2 = "res"
-TAG1 = "wp"
-UNITS = ((0, 0), (0, 1), (0, 2), (0, 3), (1, 0), (1, 1), (1, 2), (1, 3))
-Q_BYTES = ("sync", "sync", "sync", "sync")
-DEFER = 1
-EARLY = 0
-E_MEMSET = "gpsimd"
-E_PX = "svvv"
-E_W = {"w2_0": "s", "w2_1": "v", "w1_0": "v", "w1_1": "v", "w3_0": "v", "w2_2": "v", "w1_2": "v", "w2_3": "v", "w1_3": "v"}
-E_CONF = "vector"
-E_TURN = "ssvvvsvs"
-E_OUT = "ssssssss"
-LOADS = ("offs", "w2_0", "bytes", "words", "w2_1", "va", "w1_0", "vb", "unit", "sca_0_0", "w1_1", "sca_0_1", "sca_0_2", "sca_0_3", "w3_0")
+FIRST_CHUNK_DELAY = 3
+GATHERED_BUFS = 5
+STAGE_BUFS = 3
+BANKS = {"res": 3, "weight": 2, "turned": 2, "out": 1}
 
 
 def tile_picked_ydustr_grad_p_kernel(
     tc, x_words, x_scales, w1, w2, sca, unit, w3, offs, va, vb, out
 ):
     nc = tc.nc
-    engines = {"gpsimd": nc.gpsimd, "vector": nc.vector, "scalar": nc.scalar, "sync": nc.sync}
-
-    def copy_on(letter, dst, src):
-        if letter == "v":
-            nc.vector.tensor_copy(dst, src)
-        else:
-            nc.scalar.copy(dst, src)
-
     with ExitStack() as ctx:
         keep = ctx.enter_context(tc.tile_pool(name="keep", bufs=1))
-        ring = ctx.enter_context(tc.tile_pool(name="ring", bufs=RING))
-        post = ctx.enter_context(tc.tile_pool(name="post", bufs=POST))
+        ring = ctx.enter_context(tc.tile_pool(name="ring", bufs=GATHERED_BUFS))
+        stage = ctx.enter_context(tc.tile_pool(name="stage", bufs=STAGE_BUFS))
         psum = ctx.enter_context(tc.psum_pool(name="psum", bufs=1))
 
-        offs_sb = keep.tile([P, S // 16], U16, name="offs_sb")
-        va_sb = keep.tile([P, U // 16], U16, name="va_sb")
-        vb_sb = keep.tile([P, U // 16], U16, name="vb_sb")
+        def bank(role, shape):
+            return psum.tile(shape, F32, name=role, tag=role, bufs=BANKS[role])
+
+        def copy(on_scalar, dst, src):
+            if on_scalar:
+                nc.scalar.copy(dst, src)
+            else:
+                nc.vector.tensor_copy(dst, src)
+
+        offs_sb = keep.tile([P, S // LIST_ROWS], U16, name="offs_sb")
+        va_sb = keep.tile([P, U // LIST_ROWS], U16, name="va_sb")
+        vb_sb = keep.tile([P, U // LIST_ROWS], U16, name="vb_sb")
         words_all = keep.tile([P, T], I32, name="words_all", align_bytes=64)
         bytes_all = keep.tile([P, T], U8, name="bytes_all", align_bytes=64)
         unit_sb = keep.tile([P, TILES], F32, name="unit_sb")
-        engines[E_MEMSET].memset(bytes_all[:].bitcast(I32), 0)
+        nc.gpsimd.memset(bytes_all[:].bitcast(I32), 0)
 
-        starts = [sum(CHUNKS[:c]) for c in range(len(CHUNKS))]
-        pieces = {"w3_0": (w3, 0, N)}
-        for name, w, widths in (("w2", w2, PIECES2), ("w1", w1, PIECES1)):
-            for n, width in enumerate(widths):
-                pieces["%s_%d" % (name, n)] = (w, sum(widths[:n]), width)
+        def load_weight(w, col0, width, name):
+            raw = keep.tile([P, PACK, width], F32, name="raw_" + name)
+            nc.sync.dma_start(raw[:], w[:, col0 : col0 + width].rearrange("(p j) c -> p j c", j=PACK))
+            return raw
+
+        def load_sca(c, t):
+            tile = keep.tile([P, CHUNK], F32, name="sca_%d_%d" % (c, t))
+            nc.sync.dma_start(tile[:], sca[t * P : (t + 1) * P, c * CHUNK : (c + 1) * CHUNK])
+            return tile
+
         raw = {}
         sca_sb = {}
-
-        def load(name):
-            if name == "offs":
-                nc.sync.dma_start(offs_sb[:], offs)
-            elif name == "va":
-                nc.sync.dma_start(va_sb[:], va)
-            elif name == "vb":
-                nc.sync.dma_start(vb_sb[:], vb)
-            elif name == "words":
-                nc.sync.dma_start(words_all[:], x_words[0].rearrange("p n t -> p (n t)").bitcast(I32))
-            elif name == "bytes":
-                for q in range(4):
-                    engines[Q_BYTES[q]].dma_start(
-                        bytes_all[32 * q : 32 * q + 4, :].bitcast(I32), x_scales[0, 4 * q : 4 * q + 4, :].bitcast(I32)
-                    )
-            elif name == "unit":
-                with nc.allow_non_contiguous_dma(reason="one value a partition and tile"):
-                    nc.sync.dma_start(unit_sb[:], unit.rearrange("(t p) o -> p (t o)", p=P))
-            elif name in pieces:
-                w, col0, width = pieces[name]
-                raw[name] = keep.tile([P, PACK, width], F32, name="raw_" + name)
-                nc.sync.dma_start(raw[name][:], w[:, col0 : col0 + width].rearrange("(p j) c -> p j c", j=PACK))
-            else:
-                c, t = int(name.split("_")[1]), int(name.split("_")[2])
-                sca_sb[c, t] = keep.tile([P, CHUNKS[c]], F32, name=name)
-                nc.sync.dma_start(sca_sb[c, t][:], sca[t * P : (t + 1) * P, starts[c] : starts[c] + CHUNKS[c]])
-
-        for name in LOADS:
-            load(name)
-        for c, t in UNITS:
-            if (c, t) not in sca_sb:
-                load("sca_%d_%d" % (c, t))
+        nc.sync.dma_start(offs_sb[:], offs)
+        raw["w2", 0] = load_weight(w2, 0, WEIGHT_HALF, "w2_0")
+        for q in range(4):
+            nc.sync.dma_start(
+                bytes_all[32 * q : 32 * q + 4, :].bitcast(I32), x_scales[0, 4 * q : 4 * q + 4, :].bitcast(I32)
+            )
+        nc.sync.dma_start(words_all[:], x_words[0].rearrange("p n t -> p (n t)").bitcast(I32))
+        raw["w2", 1] = load_weight(w2, WEIGHT_HALF, WEIGHT_HALF, "w2_1")
+        nc.sync.dma_start(va_sb[:], va)
+        raw["w1", 0] = load_weight(w1, 0, WEIGHT_HALF, "w1_0")
+        nc.sync.dma_start(vb_sb[:], vb)
+        with nc.allow_non_contiguous_dma(reason="one value a partition and tile"):
+            nc.sync.dma_start(unit_sb[:], unit.rearrange("(t p) o -> p (t o)", p=P))
+        sca_sb[0, 0] = load_sca(0, 0)
+        raw["w1", 1] = load_weight(w1, WEIGHT_HALF, WEIGHT_HALF, "w1_1")
+        for t in range(1, TILES):
+            sca_sb[0, t] = load_sca(0, t)
+        raw["w3", 0] = load_weight(w3, 0, N, "w3_0")
+        for t in range(TILES):
+            sca_sb[1, t] = load_sca(1, t)
 
         ident = keep.tile([P, P], F32, name="ident")
         make_identity(nc, ident[:])
 
-        def window(name):
+        def table(name):
             tile = keep.tile([P, WINDOW], F32, name=name)
             nc.gpsimd.memset(tile[:, S:], 0.0)
             return tile
 
-        e_tab = [window("e_tab%d" % t) for t in range(TILES)]
-        conf_tab = [window("conf_tab%d" % t) for t in range(TILES)]
-        px_tab = [window("px_tab%d" % t) for t in range(TILES)]
+        exp_tab = [table("exp_tab%d" % t) for t in range(TILES)]
+        conf_tab = [table("conf_tab%d" % t) for t in range(TILES)]
+        px_tab = [table("px_tab%d" % t) for t in range(TILES)]
 
         x_codes = keep.tile([P, S], U32, name="x_codes", align_bytes=64)
         x_bytes = keep.tile([P, S], U8, name="x_bytes", align_bytes=64)
+        point_halves = [slice(0, S // 2), slice(S // 2, S)]
         nc.vector.tensor_copy(x_bytes[:], bytes_all[:].indirect(offs_sb[:]))
-        nc.vector.tensor_copy(x_codes[:], words_all[:].bitcast(U32).indirect(offs_sb[:]))
+        for points in point_halves:
+            picked = offs_sb[:, points.start // LIST_ROWS : points.stop // LIST_ROWS]
+            nc.vector.tensor_copy(x_codes[:, points], words_all[:].bitcast(U32).indirect(picked))
 
-        quantised = {}
-        banks = {"res": RES_BANKS, "wp": WP_BANKS, "turned": TURN_BANKS, "out": OUT_BANKS}
-
-        def quantise_weight(name):
-            width = pieces[name][2]
+        def quantise_weight(key, width):
+            name = "%s_%d" % key
             grouped = keep.tile([P, width, PACK], BF16, name="grouped_" + name, align_bytes=64)
-            copy_on(
-                E_W[name],
+            copy(
+                key == ("w2", 0),
                 grouped[:].rearrange("p (c i) j -> p c j i", i=4),
-                raw[name][:].rearrange("p j (c i) -> p c j i", i=4),
+                raw[key][:].rearrange("p j (c i) -> p c j i", i=4),
             )
             codes = keep.tile([P, width], U32, name="codes_" + name, align_bytes=64)
             scales = keep.tile([P, width], U8, name="scales_" + name, align_bytes=64)
             nc.vector.quantize_mx(
                 out=codes[:].bitcast(FP8X4), scales=scales[:], in_=grouped[:].rearrange("p c j -> p (c j)")
             )
-            quantised[name] = (codes, scales)
+            return codes, scales
 
-        def first_product(matrix, t, tag, bufs):
-            name = [n for n in pieces if n.startswith(matrix) and pieces[n][1] <= t * P < pieces[n][1] + pieces[n][2]][0]
-            if name not in quantised:
-                quantise_weight(name)
-            codes, scales = quantised[name]
-            cols = slice(t * P - pieces[name][1], (t + 1) * P - pieces[name][1])
-            acc = psum.tile([P, S], F32, name="acc", tag=tag, bufs=bufs)
+        def first_product(quantised, t, role, points):
+            codes, scales = quantised
+            cols = slice(t % 2 * P, (t % 2 + 1) * P)
+            acc = bank(role, [P, points.stop - points.start])
             nc.tensor.matmul_mx(
                 out=acc[:],
                 lhsT=codes[:, cols].bitcast(FP8X4),
                 lhsT_scale=scales[:, cols],
-                rhs=x_codes[:].bitcast(FP8X4),
-                rhs_scale=x_bytes[:],
+                rhs=x_codes[:, points].bitcast(FP8X4),
+                rhs_scale=x_bytes[:, points],
                 start=True,
                 stop=True,
             )
             return acc
 
+        quantised = {}
         for t in range(TILES):
-            cf = first_product("w2", t, TAG2, banks[TAG2])
-            th = ring.tile([P, S], F32, name="th")
-            nc.scalar.activation(th[:], cf[:], ACT.Tanh)
-            nc.scalar.activation(e_tab[t][:, :S], th[:], ACT.Exp, scale=1.2)
-            px = first_product("w1", t, TAG1, banks[TAG1])
-            copy_on(E_PX[t], px_tab[t][:, :S], px[:])
-            engines[E_CONF].tensor_scalar(
-                conf_tab[t][:, :S], e_tab[t][:, :S], 0.5, unit_sb[:, t : t + 1], ALU.add, ALU.mult
-            )
-        quantise_weight("w3_0")
-        w3_codes, w3_scales = quantised["w3_0"]
+            half = t // 2
+            bounded = ring.tile([P, S], F32, name="bounded")
+            if t % 2 == 0:
+                quantised["w2", half] = quantise_weight(("w2", half), WEIGHT_HALF)
+            for points in point_halves if t == 0 else [slice(0, S)]:
+                cf = first_product(quantised["w2", half], t, "res", points)
+                nc.scalar.activation(bounded[:, points], cf[:], ACT.Tanh)
+            nc.scalar.activation(exp_tab[t][:, :S], bounded[:], ACT.Exp, scale=1.2)
+            if t % 2 == 0:
+                quantised["w1", half] = quantise_weight(("w1", half), WEIGHT_HALF)
+            px = first_product(quantised["w1", half], t, "weight", slice(0, S))
+            copy(t == 0, px_tab[t][:, :S], px[:])
+            nc.vector.tensor_scalar(conf_tab[t][:, :S], exp_tab[t][:, :S], 0.5, unit_sb[:, t : t + 1], ALU.add, ALU.mult)
+        w3_codes, w3_scales = quantise_weight(("w3", 0), N)
 
-        units = list(UNITS)
-        spans = [CHUNKS[c] if c < len(CHUNKS) - 1 else HID_SPAN for c in range(len(CHUNKS))]
+        cells = [(c, t) for c in range(CHUNKS) for t in range(TILES)]
+        last_chunk = CHUNKS - 1
+        span = [HALF if c == last_chunk else CHUNK for c in range(CHUNKS)]
         hid_t = {}
-        for c in range(len(CHUNKS)):
-            for col0 in range(0, CHUNKS[c], spans[c]):
-                hid_t[c, col0] = keep.tile([P, spans[c] // P, H], BF16, name="hid_t%d_%d" % (c, col0))
-        state = {}
-        waiting = []
+        for c in range(CHUNKS):
+            for col0 in range(0, CHUNK, span[c]):
+                hid_t[c, col0] = keep.tile([P, span[c] // P, H], BF16, name="hid_t%d_%d" % (c, col0))
+        made = {}
 
         def entries(lst, c):
-            return lst[:, starts[c] // 16 : (starts[c] + CHUNKS[c]) // 16]
+            return lst[:, c * CHUNK // LIST_ROWS : (c + 1) * CHUNK // LIST_ROWS]
 
-        def fetch_a(k):
-            c, t = units[k]
-            ca = ring.tile([P, CHUNKS[c]], F32, name="ca")
-            nc.scalar.activation(ca[:], e_tab[t][:].indirect(entries(va_sb, c)), ACT.Copy, bias=0.5)
-            sxa = ring.tile([P, CHUNKS[c]], F32, name="sxa")
-            nc.vector.tensor_tensor(sxa[:], px_tab[t][:].indirect(entries(va_sb, c)), sca_sb[c, t][:], ALU.mult)
-            state["ca", k], state["sxa", k] = ca, sxa
+        def gather_by_va(k):
+            c, t = cells[k]
+            ca = ring.tile([P, CHUNK], F32, name="ca")
+            nc.scalar.activation(ca[:], exp_tab[t][:].indirect(entries(va_sb, c)), ACT.Copy, bias=0.5)
+            scaled_xa = ring.tile([P, CHUNK], F32, name="scaled_xa")
+            nc.vector.tensor_tensor(scaled_xa[:], px_tab[t][:].indirect(entries(va_sb, c)), sca_sb[c, t][:], ALU.mult)
+            made["ca", k], made["scaled_xa", k] = ca, scaled_xa
 
-        def fetch_b(k):
-            c, t = units[k]
-            nxb = ring.tile([P, CHUNKS[c]], F32, name="nxb")
-            nc.scalar.activation(nxb[:], px_tab[t][:].indirect(entries(vb_sb, c)), ACT.Copy, scale=-1.0)
-            wp = ring.tile([P, CHUNKS[c]], F32, name="wp")
-            nc.vector.tensor_tensor(wp[:], conf_tab[t][:].indirect(entries(vb_sb, c)), state["ca", k][:], ALU.mult)
-            state["wp", k], state["nxb", k] = wp, nxb
+        def gather_by_vb(k):
+            c, t = cells[k]
+            minus_xb = ring.tile([P, CHUNK], F32, name="minus_xb")
+            nc.scalar.activation(minus_xb[:], px_tab[t][:].indirect(entries(vb_sb, c)), ACT.Copy, scale=-1.0)
+            weight = ring.tile([P, CHUNK], F32, name="weight")
+            nc.vector.tensor_tensor(weight[:], conf_tab[t][:].indirect(entries(vb_sb, c)), made["ca", k][:], ALU.mult)
+            made["weight", k], made["minus_xb", k] = weight, minus_xb
 
         def parts(k):
-            width = CHUNKS[units[k][0]]
-            piece = LAST_PIECE if k >= len(units) - SPLIT else width
-            return [(k, col0, min(piece, width - col0)) for col0 in range(0, width, piece)]
+            width = HALF if k == len(cells) - 1 else CHUNK
+            return [(k, col0, width) for col0 in range(0, CHUNK, width)]
 
-        def turn_res(part):
+        def turn_residual(part):
             k, col0, width = part
-            res = psum.tile([P, width], F32, name="res", tag="res", bufs=RES_BANKS)
+            res = bank("res", [P, width])
             for b in range(width // P):
-                cols = slice(b * P, (b + 1) * P)
+                dst = res[:, b * P : (b + 1) * P]
                 src = slice(col0 + b * P, col0 + (b + 1) * P)
-                nc.tensor.matmul(res[:, cols], state["sxa", k][:, src], ident[:], start=True, stop=False, is_transpose=True)
-                nc.tensor.matmul(res[:, cols], state["nxb", k][:, src], ident[:], start=False, stop=True, is_transpose=True)
-            state["res", part] = res
+                nc.tensor.matmul(dst, made["scaled_xa", k][:, src], ident[:], start=True, stop=False, is_transpose=True)
+                nc.tensor.matmul(dst, made["minus_xb", k][:, src], ident[:], start=False, stop=True, is_transpose=True)
+            made["res", part] = res
 
-        def turn_wp(part):
+        def turn_weight(part):
             k, col0, width = part
-            wp_t = psum.tile([P, width], F32, name="wp_t", tag="wp", bufs=WP_BANKS)
+            weight_t = bank("weight", [P, width])
             for b in range(width // P):
-                nc.tensor.transpose(wp_t[:, b * P : (b + 1) * P], state["wp", k][:, col0 + b * P : col0 + (b + 1) * P], ident[:])
-            state["wp_t", part] = wp_t
+                src = slice(col0 + b * P, col0 + (b + 1) * P)
+                nc.tensor.transpose(weight_t[:, b * P : (b + 1) * P], made["weight", k][:, src], ident[:])
+            made["weight_t", part] = weight_t
 
         def square(part):
-            sq = post.tile([P, part[2]], F32, name="sq")
-            nc.scalar.activation(sq[:], state["res", part][:], ACT.Square)
-            state["sq", part] = sq
+            squared = stage.tile([P, part[2]], F32, name="squared")
+            nc.scalar.activation(squared[:], made["res", part][:], ACT.Square)
+            made["squared", part] = squared
 
         def inverse_root(part):
-            rs = post.tile([P, part[2]], F32, name="rs")
-            nc.scalar.activation(rs[:], state["sq", part][:], ACT.Abs_reciprocal_sqrt, bias=0.3)
-            state["rs", part] = rs
+            root = stage.tile([P, part[2]], F32, name="root")
+            nc.scalar.activation(root[:], made["squared", part][:], ACT.Abs_reciprocal_sqrt, bias=0.3)
+            made["root", part] = root
 
-        def huber(part):
-            hub = post.tile([P, part[2]], F32, name="hub")
-            nc.vector.tensor_tensor(hub[:], state["res", part][:], state["rs", part][:], ALU.mult)
-            state["hub", part] = hub
+        def clip(part):
+            hub = stage.tile([P, part[2]], F32, name="hub")
+            nc.vector.tensor_tensor(hub[:], made["res", part][:], made["root", part][:], ALU.mult)
+            made["hub", part] = hub
 
         def hidden(part):
             k, col0, width = part
-            c, t = units[k]
-            step = min(width, spans[c])
-            for at in range(0, width, step):
-                base = (col0 + at) // spans[c] * spans[c]
-                first = (col0 + at - base) // P
+            c, t = cells[k]
+            for at in range(0, width, span[c]):
+                cols = slice(at, at + span[c])
                 nc.vector.tensor_tensor(
-                    hid_t[c, base][:, first : first + step // P, t * P : (t + 1) * P],
-                    state["wp_t", part][:, at : at + step].rearrange("p (b i) -> p b i", i=P),
-                    state["hub", part][:, at : at + step].rearrange("p (b i) -> p b i", i=P),
+                    hid_t[c, col0 + at][:, :, t * P : (t + 1) * P],
+                    made["weight_t", part][:, cols].rearrange("p (b i) -> p b i", i=P),
+                    made["hub", part][:, cols].rearrange("p (b i) -> p b i", i=P),
                     ALU.mult,
                 )
 
-        def finish(part):
-            k, col0, width = part
-            c, t = units[k]
-            if t == TILES - 1:
-                group = GROUP if c < len(CHUNKS) - 1 else LAST_GROUP
-                for g0 in range(col0, col0 + width, group):
-                    if c < len(CHUNKS) - 1:
-                        waiting.append((k + DEFER, c, g0, min(group, col0 + width - g0)))
-                    else:
-                        last_product(c, g0, min(group, col0 + width - g0))
-
-        def last_product(c, col0, width):
-            group = (starts[c] + col0) // P
+        def last_product(c, col0, width, turn_role, out_role, turn_on_scalar):
             blocks = width // P
-            tag_turn, tag_out = TAGS_LAST if c == len(CHUNKS) - 1 else TAGS_FIRST
+            tile_col0 = col0 // span[c] * span[c]
             grouped = ring.tile([P, width, PACK], BF16, name="hid_grouped", align_bytes=64)
             grouped_words = grouped[:].rearrange("p r j -> p (r j)").bitcast(F32)
-            turned = psum.tile([P, blocks, 2, P], F32, name="turned", tag=tag_turn, bufs=banks[tag_turn])
+            turned = bank(turn_role, [P, blocks, 2, P])
             for b in range(blocks):
-                base = col0 // spans[c] * spans[c]
-                words = hid_t[c, base][:, (col0 - base) // P + b, :].bitcast(F32)
+                pairs = hid_t[c, tile_col0][:, (col0 - tile_col0) // P + b, :].bitcast(F32)
                 for u in range(2):
-                    nc.tensor.transpose(turned[:, b, u, :], words[:, u::2], ident[:])
-            copy_on(
-                E_TURN[group],
+                    nc.tensor.transpose(turned[:, b, u, :], pairs[:, u::2], ident[:])
+            copy(
+                turn_on_scalar,
                 grouped_words.rearrange("p (b r u) -> p b r u", b=blocks, u=2),
                 turned[:].rearrange("p b u r -> p b r u"),
             )
@@ -301,7 +259,7 @@ def tile_picked_ydustr_grad_p_kernel(
             nc.vector.quantize_mx(
                 out=codes[:].bitcast(FP8X4), scales=scales[:], in_=grouped[:].rearrange("p r j -> p (r j)")
             )
-            acc = psum.tile([P, width], F32, name="out_acc", tag=tag_out, bufs=banks[tag_out])
+            acc = bank(out_role, [P, width])
             nc.tensor.matmul_mx(
                 out=acc[:],
                 lhsT=w3_codes[:].bitcast(FP8X4),
@@ -312,34 +270,32 @@ def tile_picked_ydustr_grad_p_kernel(
                 stop=True,
             )
             result = ring.tile([P, width], F32, name="result")
-            copy_on(E_OUT[group], result[:], acc[:])
-            nc.sync.dma_start(out[:, starts[c] + col0 : starts[c] + col0 + width], result[:])
+            nc.scalar.copy(result[:], acc[:])
+            nc.sync.dma_start(out[:, c * CHUNK + col0 : c * CHUNK + col0 + width], result[:])
 
-        count = len(units)
-
-        def each(stage, k):
-            if 0 <= k < count:
+        def each(work, k):
+            if 0 <= k < len(cells):
                 for part in parts(k):
-                    stage(part)
+                    work(part)
 
-        for step in range(count + LAG_HID):
-            if step < count:
-                fetch_a(step)
-            each(turn_res, step - LAG_RES)
-            each(square, step - LAG_SQ)
-            each(huber, step - LAG_HUB)
-            if step < count:
-                fetch_b(step)
-            each(turn_wp, step - LAG_WP)
-            each(inverse_root, step - LAG_SQ)
-            for item in list(waiting):
-                if item[0] <= step - LAG_HID + EARLY:
-                    waiting.remove(item)
-                    last_product(*item[1:])
-            if TOGETHER:
-                each(hidden, step - LAG_HID)
-                each(finish, step - LAG_HID)
-            elif 0 <= step - LAG_HID < count:
-                for part in parts(step - LAG_HID):
-                    hidden(part)
-                    finish(part)
+        def hidden_and_end(part):
+            hidden(part)
+            k, col0, width = part
+            if k == len(cells) - 1:
+                for block0 in range(col0, col0 + width, P):
+                    last_product(last_chunk, block0, P, "res", "weight", block0 // P % 2 == 1)
+
+        for step in range(len(cells) + LAG_HID):
+            if step < len(cells):
+                gather_by_va(step)
+            each(turn_residual, step - LAG_ROOT)
+            each(square, step - LAG_ROOT)
+            each(clip, step - LAG_CLIP)
+            if step < len(cells):
+                gather_by_vb(step)
+            each(turn_weight, step - LAG_CLIP)
+            each(inverse_root, step - LAG_ROOT)
+            if step == TILES - 1 + LAG_HID + FIRST_CHUNK_DELAY:
+                for col0 in range(0, CHUNK, HALF):
+                    last_product(0, col0, HALF, "turned", "out", True)
+            each(hidden_and_end, step - LAG_HID)

from contextlib import ExitStack

import concourse.mybir as mybir
from concourse.masks import make_identity

K, T, S, N, H, U = 512, 2048, 512, 128, 512, 1024
FLOPS = 2 * K * H * S * 2 + 2 * H * N * U

F32 = mybir.dt.float32
BF16 = mybir.dt.bfloat16
I32 = mybir.dt.int32
U32 = mybir.dt.uint32
U16 = mybir.dt.uint16
U8 = mybir.dt.uint8
FP8X4 = mybir.dt.float8_e4m3fn_x4
ACT = mybir.ActivationFunctionType
ALU = mybir.AluOpType

P = 128
PACK = 4
LIST_ROWS = 16
TILES = H // P
CHUNK = 512
CHUNKS = U // CHUNK
HALF = CHUNK // 2
WEIGHT_HALF = H // 2
WINDOW = S + 16

LAG_ROOT = 1
LAG_CLIP = 2
LAG_HID = 3
FIRST_CHUNK_DELAY = 3
GATHERED_BUFS = 5
STAGE_BUFS = 3
BANKS = {"res": 3, "weight": 2, "turned": 2, "out": 1}


def tile_picked_ydustr_grad_p_kernel(
    tc, x_words, x_scales, w1, w2, sca, unit, w3, offs, va, vb, out
):
    nc = tc.nc
    with ExitStack() as ctx:
        keep = ctx.enter_context(tc.tile_pool(name="keep", bufs=1))
        ring = ctx.enter_context(tc.tile_pool(name="ring", bufs=GATHERED_BUFS))
        stage = ctx.enter_context(tc.tile_pool(name="stage", bufs=STAGE_BUFS))
        psum = ctx.enter_context(tc.psum_pool(name="psum", bufs=1))

        def bank(role, shape):
            return psum.tile(shape, F32, name=role, tag=role, bufs=BANKS[role])

        def copy(on_scalar, dst, src):
            if on_scalar:
                nc.scalar.copy(dst, src)
            else:
                nc.vector.tensor_copy(dst, src)

        offs_sb = keep.tile([P, S // LIST_ROWS], U16, name="offs_sb")
        va_sb = keep.tile([P, U // LIST_ROWS], U16, name="va_sb")
        vb_sb = keep.tile([P, U // LIST_ROWS], U16, name="vb_sb")
        words_all = keep.tile([P, T], I32, name="words_all", align_bytes=64)
        bytes_all = keep.tile([P, T], U8, name="bytes_all", align_bytes=64)
        unit_sb = keep.tile([P, TILES], F32, name="unit_sb")
        nc.gpsimd.memset(bytes_all[:].bitcast(I32), 0)

        def load_weight(w, col0, width, name):
            raw = keep.tile([P, PACK, width], F32, name="raw_" + name)
            nc.sync.dma_start(raw[:], w[:, col0 : col0 + width].rearrange("(p j) c -> p j c", j=PACK))
            return raw

        def load_sca(c, t):
            tile = keep.tile([P, CHUNK], F32, name="sca_%d_%d" % (c, t))
            nc.sync.dma_start(tile[:], sca[t * P : (t + 1) * P, c * CHUNK : (c + 1) * CHUNK])
            return tile

        raw = {}
        sca_sb = {}
        nc.sync.dma_start(offs_sb[:], offs)
        raw["w2", 0] = load_weight(w2, 0, WEIGHT_HALF, "w2_0")
        for q in range(4):
            nc.sync.dma_start(
                bytes_all[32 * q : 32 * q + 4, :].bitcast(I32), x_scales[0, 4 * q : 4 * q + 4, :].bitcast(I32)
            )
        nc.sync.dma_start(words_all[:], x_words[0].rearrange("p n t -> p (n t)").bitcast(I32))
        raw["w2", 1] = load_weight(w2, WEIGHT_HALF, WEIGHT_HALF, "w2_1")
        nc.sync.dma_start(va_sb[:], va)
        raw["w1", 0] = load_weight(w1, 0, WEIGHT_HALF, "w1_0")
        nc.sync.dma_start(vb_sb[:], vb)
        with nc.allow_non_contiguous_dma(reason="one value a partition and tile"):
            nc.sync.dma_start(unit_sb[:], unit.rearrange("(t p) o -> p (t o)", p=P))
        sca_sb[0, 0] = load_sca(0, 0)
        raw["w1", 1] = load_weight(w1, WEIGHT_HALF, WEIGHT_HALF, "w1_1")
        for t in range(1, TILES):
            sca_sb[0, t] = load_sca(0, t)
        raw["w3", 0] = load_weight(w3, 0, N, "w3_0")
        for t in range(TILES):
            sca_sb[1, t] = load_sca(1, t)

        ident = keep.tile([P, P], F32, name="ident")
        make_identity(nc, ident[:])

        def table(name):
            tile = keep.tile([P, WINDOW], F32, name=name)
            nc.gpsimd.memset(tile[:, S:], 0.0)
            return tile

        exp_tab = [table("exp_tab%d" % t) for t in range(TILES)]
        conf_tab = [table("conf_tab%d" % t) for t in range(TILES)]
        px_tab = [table("px_tab%d" % t) for t in range(TILES)]

        x_codes = keep.tile([P, S], U32, name="x_codes", align_bytes=64)
        x_bytes = keep.tile([P, S], U8, name="x_bytes", align_bytes=64)
        point_halves = [slice(0, S // 2), slice(S // 2, S)]
        nc.vector.tensor_copy(x_bytes[:], bytes_all[:].indirect(offs_sb[:]))
        for points in point_halves:
            picked = offs_sb[:, points.start // LIST_ROWS : points.stop // LIST_ROWS]
            nc.vector.tensor_copy(x_codes[:, points], words_all[:].bitcast(U32).indirect(picked))

        def quantise_weight(key, width):
            name = "%s_%d" % key
            grouped = keep.tile([P, width, PACK], BF16, name="grouped_" + name, align_bytes=64)
            copy(
                key == ("w2", 0),
                grouped[:].rearrange("p (c i) j -> p c j i", i=4),
                raw[key][:].rearrange("p j (c i) -> p c j i", i=4),
            )
            codes = keep.tile([P, width], U32, name="codes_" + name, align_bytes=64)
            scales = keep.tile([P, width], U8, name="scales_" + name, align_bytes=64)
            nc.vector.quantize_mx(
                out=codes[:].bitcast(FP8X4), scales=scales[:], in_=grouped[:].rearrange("p c j -> p (c j)")
            )
            return codes, scales

        def first_product(quantised, t, role, points):
            codes, scales = quantised
            cols = slice(t % 2 * P, (t % 2 + 1) * P)
            acc = bank(role, [P, points.stop - points.start])
            nc.tensor.matmul_mx(
                out=acc[:],
                lhsT=codes[:, cols].bitcast(FP8X4),
                lhsT_scale=scales[:, cols],
                rhs=x_codes[:, points].bitcast(FP8X4),
                rhs_scale=x_bytes[:, points],
                start=True,
                stop=True,
            )
            return acc

        quantised = {}
        for t in range(TILES):
            half = t // 2
            bounded = ring.tile([P, S], F32, name="bounded")
            if t % 2 == 0:
                quantised["w2", half] = quantise_weight(("w2", half), WEIGHT_HALF)
            for points in point_halves if t == 0 else [slice(0, S)]:
                cf = first_product(quantised["w2", half], t, "res", points)
                nc.scalar.activation(bounded[:, points], cf[:], ACT.Tanh)
            nc.scalar.activation(exp_tab[t][:, :S], bounded[:], ACT.Exp, scale=1.2)
            if t % 2 == 0:
                quantised["w1", half] = quantise_weight(("w1", half), WEIGHT_HALF)
            px = first_product(quantised["w1", half], t, "weight", slice(0, S))
            copy(t == 0, px_tab[t][:, :S], px[:])
            nc.vector.tensor_scalar(conf_tab[t][:, :S], exp_tab[t][:, :S], 0.5, unit_sb[:, t : t + 1], ALU.add, ALU.mult)
        w3_codes, w3_scales = quantise_weight(("w3", 0), N)

        cells = [(c, t) for c in range(CHUNKS) for t in range(TILES)]
        last_chunk = CHUNKS - 1
        span = [HALF if c == last_chunk else CHUNK for c in range(CHUNKS)]
        hid_t = {}
        for c in range(CHUNKS):
            for col0 in range(0, CHUNK, span[c]):
                hid_t[c, col0] = keep.tile([P, span[c] // P, H], BF16, name="hid_t%d_%d" % (c, col0))
        made = {}

        def entries(lst, c):
            return lst[:, c * CHUNK // LIST_ROWS : (c + 1) * CHUNK // LIST_ROWS]

        def gather_by_va(k):
            c, t = cells[k]
            ca = ring.tile([P, CHUNK], F32, name="ca")
            nc.scalar.activation(ca[:], exp_tab[t][:].indirect(entries(va_sb, c)), ACT.Copy, bias=0.5)
            scaled_xa = ring.tile([P, CHUNK], F32, name="scaled_xa")
            nc.vector.tensor_tensor(scaled_xa[:], px_tab[t][:].indirect(entries(va_sb, c)), sca_sb[c, t][:], ALU.mult)
            made["ca", k], made["scaled_xa", k] = ca, scaled_xa

        def gather_by_vb(k):
            c, t = cells[k]
            minus_xb = ring.tile([P, CHUNK], F32, name="minus_xb")
            nc.scalar.activation(minus_xb[:], px_tab[t][:].indirect(entries(vb_sb, c)), ACT.Copy, scale=-1.0)
            weight = ring.tile([P, CHUNK], F32, name="weight")
            nc.vector.tensor_tensor(weight[:], conf_tab[t][:].indirect(entries(vb_sb, c)), made["ca", k][:], ALU.mult)
            made["weight", k], made["minus_xb", k] = weight, minus_xb

        def parts(k):
            width = HALF if k == len(cells) - 1 else CHUNK
            return [(k, col0, width) for col0 in range(0, CHUNK, width)]

        def turn_residual(part):
            k, col0, width = part
            res = bank("res", [P, width])
            for b in range(width // P):
                dst = res[:, b * P : (b + 1) * P]
                src = slice(col0 + b * P, col0 + (b + 1) * P)
                nc.tensor.matmul(dst, made["scaled_xa", k][:, src], ident[:], start=True, stop=False, is_transpose=True)
                nc.tensor.matmul(dst, made["minus_xb", k][:, src], ident[:], start=False, stop=True, is_transpose=True)
            made["res", part] = res

        def turn_weight(part):
            k, col0, width = part
            weight_t = bank("weight", [P, width])
            for b in range(width // P):
                src = slice(col0 + b * P, col0 + (b + 1) * P)
                nc.tensor.transpose(weight_t[:, b * P : (b + 1) * P], made["weight", k][:, src], ident[:])
            made["weight_t", part] = weight_t

        def square(part):
            squared = stage.tile([P, part[2]], F32, name="squared")
            nc.scalar.activation(squared[:], made["res", part][:], ACT.Square)
            made["squared", part] = squared

        def inverse_root(part):
            root = stage.tile([P, part[2]], F32, name="root")
            nc.scalar.activation(root[:], made["squared", part][:], ACT.Abs_reciprocal_sqrt, bias=0.3)
            made["root", part] = root

        def clip(part):
            hub = stage.tile([P, part[2]], F32, name="hub")
            nc.vector.tensor_tensor(hub[:], made["res", part][:], made["root", part][:], ALU.mult)
            made["hub", part] = hub

        def hidden(part):
            k, col0, width = part
            c, t = cells[k]
            for at in range(0, width, span[c]):
                cols = slice(at, at + span[c])
                nc.vector.tensor_tensor(
                    hid_t[c, col0 + at][:, :, t * P : (t + 1) * P],
                    made["weight_t", part][:, cols].rearrange("p (b i) -> p b i", i=P),
                    made["hub", part][:, cols].rearrange("p (b i) -> p b i", i=P),
                    ALU.mult,
                )

        def last_product(c, col0, width, turn_role, out_role, turn_on_scalar):
            blocks = width // P
            tile_col0 = col0 // span[c] * span[c]
            grouped = ring.tile([P, width, PACK], BF16, name="hid_grouped", align_bytes=64)
            grouped_words = grouped[:].rearrange("p r j -> p (r j)").bitcast(F32)
            turned = bank(turn_role, [P, blocks, 2, P])
            for b in range(blocks):
                pairs = hid_t[c, tile_col0][:, (col0 - tile_col0) // P + b, :].bitcast(F32)
                for u in range(2):
                    nc.tensor.transpose(turned[:, b, u, :], pairs[:, u::2], ident[:])
            copy(
                turn_on_scalar,
                grouped_words.rearrange("p (b r u) -> p b r u", b=blocks, u=2),
                turned[:].rearrange("p b u r -> p b r u"),
            )
            codes = ring.tile([P, width], U32, name="hid_codes", align_bytes=64)
            scales = ring.tile([P, width], U8, name="hid_scales", align_bytes=64)
            nc.vector.quantize_mx(
                out=codes[:].bitcast(FP8X4), scales=scales[:], in_=grouped[:].rearrange("p r j -> p (r j)")
            )
            acc = bank(out_role, [P, width])
            nc.tensor.matmul_mx(
                out=acc[:],
                lhsT=w3_codes[:].bitcast(FP8X4),
                lhsT_scale=w3_scales[:],
                rhs=codes[:].bitcast(FP8X4),
                rhs_scale=scales[:],
                start=True,
                stop=True,
            )
            result = ring.tile([P, width], F32, name="result")
            nc.scalar.copy(result[:], acc[:])
            nc.sync.dma_start(out[:, c * CHUNK + col0 : c * CHUNK + col0 + width], result[:])

        def each(work, k):
            if 0 <= k < len(cells):
                for part in parts(k):
                    work(part)

        def hidden_and_end(part):
            hidden(part)
            k, col0, width = part
            if k == len(cells) - 1:
                for block0 in range(col0, col0 + width, P):
                    last_product(last_chunk, block0, P, "res", "weight", block0 // P % 2 == 1)

        for step in range(len(cells) + LAG_HID):
            if step < len(cells):
                gather_by_va(step)
            each(turn_residual, step - LAG_ROOT)
            each(square, step - LAG_ROOT)
            each(clip, step - LAG_CLIP)
            if step < len(cells):
                gather_by_vb(step)
            each(turn_weight, step - LAG_CLIP)
            each(inverse_root, step - LAG_ROOT)
            if step == TILES - 1 + LAG_HID + FIRST_CHUNK_DELAY:
                for col0 in range(0, CHUNK, HALF):
                    last_product(0, col0, HALF, "turned", "out", True)
            each(hidden_and_end, step - LAG_HID)
